import numpy as np, ml_dtypes
CORES = [3,7,11,15,131,135,139,143]
N = 8
BF = ml_dtypes.bfloat16
L, S, NR, NC, RO, ST = 256, 8, 2048, 512, 4, 5
def kill(rng, R, share):
    return np.where(rng.random((N, 8, 1, NR)) < share, 64, R)
def shares(rng):
    return np.stack([rng.permutation(np.array([0.1, 0.3, 0.3, 0.5, 0.5, 0.7, 0.7, 0.85])) for q in range(N)])[:, :, None, None]
def parts(rng):
    a = rng.choice(np.array([0.3, 1.0]), (N, 8, 1, NR))
    R = np.clip((16 + 32 * a * (rng.random((N, 8, 16, NR)) - 0.5)).astype(np.int64), 0, 31)
    H = rng.integers(90, 180, (N, 8, RO)) - 12 * np.arange(RO)
    return (rng.integers(0, 256, (N, 8, 16)), kill(rng, R, shares(rng)), rng.integers(0, NR, (N, 8, 16, NC)), rng.integers(0, 4096, (N, 8, NR)),
            rng.integers(0, 32, (N, 8, 16, L)), rng.integers(0, 4096, (N, 8, L)), np.maximum(H, 0))
def pack(w, R, C, P, Z, F, H):
    i = lambda a, *s: np.ascontiguousarray(a.reshape(*s)).astype(np.int32)
    return {"rec": np.ascontiguousarray(R.reshape(N, 128, NR)).astype(np.float32).astype(BF), "cel": i(C, N, 128, NC), "po": i(P, N, 8, NR),
            "pat": np.ascontiguousarray(Z.reshape(N, 128, L)).astype(np.float32).astype(BF), "phi": i(F, N, 8, L), "th": i(H, N, 8, RO), "wt": i(w, N, 128, 1)}
def lowest(ok, c):
    first = np.full((8, NC), L); lane = np.arange(L)[None, :]; g = np.arange(8)[:, None]
    np.minimum.at(first, (np.broadcast_to(g, c.shape), c), np.where(ok, lane, L))
    return ok & (first[g, c] == lane)
def look(R, C, Z, c):
    s = np.take_along_axis(C, c[:, None, :], 2)
    v = np.take_along_axis(R, s.reshape(8, 1, 16 * L), 2).reshape(8, 16, 16, L)
    return s, np.sum(np.abs(v - Z[:, :, None, :]), axis=1), v[:, 0] < 64
def at(a, k):
    return np.take_along_axis(a, k[:, None, :], 1)[:, 0]
def visit(R, C, P, Z, F, w, h, t):
    h1 = h[:, None, None]
    u = np.sum(w[:, :, None] * Z, axis=1) & 4095
    c = ((F * u >> 5) + F + 77 * t) & (NC - 1); e = ((c * u >> 5) + c + 1) & (NC - 1)
    s, d, live = look(R, C, Z, c); s2, d2, live2 = look(R, C, Z, e)
    sup = live & (d < h1); riv = live & (d >= h1)
    gain = 4 * np.sum(np.where(sup, h1 - d, 0), axis=1); loss = np.sum(np.where(riv, d - h1, 0), axis=1)
    acc = lowest(gain >= loss, c)
    has = np.any(sup, axis=1); y = np.argmin(np.where(sup, d, 9999), axis=1); ny = at(s, y)
    foe = np.any(riv, axis=1); nv = at(s, np.argmax(np.where(riv, d, -1), axis=1))
    zn = np.where(has[:, None, :], (Z + np.take_along_axis(R, ny[:, None, :], 2)) >> 1, Z)
    fn = np.where(acc & has, (np.take_along_axis(P, ny, 1) + 5 * at(d, y) + F) & 4095, (5 * F + u) & 4095)
    n = S * np.arange(L)[None, :] + (u & (S - 1))
    R2 = R.copy(); C2 = C.copy(); P2 = P.copy()
    g, i = np.nonzero(acc & foe); R2[g, :, nv[g, i]] = 64
    g, i = np.nonzero(acc); R2[g, :, n[g, i]] = zn[g, :, i]; P2[g, n[g, i]] = fn[g, i]
    g, i = np.nonzero(acc & np.any(~live, axis=1)); row = np.argmax(~live, axis=1)
    C2[g, row[g, i], c[g, i]] = n[g, i]
    acc2 = lowest(acc & ~np.any(live2 & (d2 < h1), axis=1), e)
    g, i = np.nonzero(acc2 & np.any(~live2, axis=1)); row = 15 - np.argmax(~live2[:, ::-1], axis=1)
    C2[g, row[g, i], e[g, i]] = n[g, i]
    return R2, C2, P2, zn, fn, acc
def setup_inputs(rng):
    return pack(*parts(rng))
def setup_inputs_spread(rng):
    w, R, C, P, Z, F, H = parts(rng)
    R = np.minimum((32 * rng.random((N, 8, 16, NR)) ** np.exp2(rng.integers(-2, 3, (N, 8, 1, NR)))).astype(np.int64), 31)
    Z = np.minimum((32 * rng.random((N, 8, 16, L)) ** np.exp2(rng.integers(-2, 3, (N, 8, 1, L)))).astype(np.int64), 31)
    C = np.minimum((NR * rng.random((N, 8, 16, NC)) ** 3).astype(np.int64), NR - 1)
    P = np.minimum(np.exp2(12 * rng.random((N, 8, NR))).astype(np.int64), 4095); F = np.minimum(np.exp2(12 * rng.random((N, 8, L))).astype(np.int64), 4095)
    w = np.minimum(np.exp2(8 * rng.random((N, 8, 16))).astype(np.int64), 255)
    H = np.where(rng.random((N, 8, RO)) < 0.6, rng.integers(60, 220, (N, 8, RO)), rng.integers(0, 481, (N, 8, RO)))
    return pack(w, kill(rng, R, shares(rng)), C, P, Z, F, H)
def edge(rng, n):
    k = rng.integers(0, 4, (N, 8, 1, n))
    return 31 * np.where(k <= 1, 0, np.where(k == 2, 1, rng.integers(0, 2, (N, 8, 16, n))))
def setup_inputs_ends(rng):
    w = 255 * rng.integers(0, 2, (N, 8, 16)); R = kill(rng, edge(rng, NR), 0.4); Z = edge(rng, L)
    C = np.where(rng.random((N, 8, 16, NC)) < 0.7, (NR - 1) * rng.integers(0, 2, (N, 8, 16, NC)), rng.integers(0, NR, (N, 8, 16, NC)))
    P = 4095 * rng.integers(0, 2, (N, 8, NR)); F = 4095 * rng.integers(0, 2, (N, 8, L)); H = 480 * rng.integers(0, 2, (N, 8, RO))
    for q in range(N):
        for g in range(6):
            R[q, g, :, 0] = (0, 31, 64)[(q + g) % 3]; R[q, g, :, NR - 1] = (0, 31, 64)[(q + g + 1) % 3]
    w[:, 5] = 0; w[:, 5, 0] = 195; Z[:, 5, 0, 0] = 21; F[:, 5, 0] = 4095
    R[:, 6] = 64; Z[:, 6] = 0; F[:, 6] = 0
    H[:, 7, 0] = 0; H[:, 7, 1] = 480; R[:, 7, :, 0] = 31; R[:, 7, :, NR - 1] = 0
    C[:, 7, :, 0] = 0; C[:, 7, :, NC - 1] = 0; C[:, 7, :, 77] = NR - 1
    for k in (0, 5, L - 2, L - 1):
        Z[:, 7, :, k] = 0; F[:, 7, k] = 0
    for q in range(N):
        a = visit(R[q], C[q], P[q], Z[q], F[q], w[q], H[q, :, 0], 0)[5]; a[6] = False
        m = 1 + ((30 - int(np.count_nonzero(a))) & 31)
        F[q, 6, rng.permutation(L)[:m - 1]] = np.arange(1, m)
    return pack(w, R, C, P, Z, F, H)
def selfsame(rng, u0, p0):
    p = np.arange(4096)[:, None]; u = np.arange(256)[None, :]
    c = ((p * u >> 5) + p) & (NC - 1); e = ((c * u >> 5) + c + 1) & (NC - 1)
    c0 = ((p0 * u0 >> 5) + p0) & (NC - 1); e0 = ((c0 * u0 >> 5) + c0 + 1) & (NC - 1)
    i, j = np.nonzero((c == e) & (c != c0) & (c != e0)); z = int(rng.integers(0, len(i)))
    return int(j[z]), int(i[z])
def setup_inputs_corners(rng):
    w, R, C, P, Z, F, H = parts(rng)
    for q in range(N):
        for g in range(8):
            o = (g + q) & 7
            if o == 0:
                R[q, g] = 64; Z[q, g] = 0; F[q, g] = rng.permutation(NC)[:L]
                w[q, g] = 0; w[q, g, 0] = 163; Z[q, g, 0, 0] = 25; F[q, g, 0] = 4093
                u, p = selfsame(rng, 4075, 4093)
                w[q, g, 1] = 1; w[q, g, 2] = 32; Z[q, g, 1, 1] = u & 31; Z[q, g, 2, 1] = u >> 5; F[q, g, 1] = p
            elif o == 1:
                R[q, g] = rng.integers(0, 32, (16, NR))
            elif o == 2:
                h = NR // 2; R[q, g, :, :h] = rng.integers(0, 32, (16, h)); R[q, g, :, h:] = 64
                C[q, g] = rng.integers(0, h, (16, NC)) + h * (np.arange(NC) & 1)[None, :]
                C[q, g, 15, 2::4] = h + rng.integers(0, h, NC // 4); C[q, g, 0, 3::4] = rng.integers(0, h, NC // 4)
            elif o == 3:
                C[q, g] = rng.integers(0, NR, (1, NC))
            elif o == 4:
                w[q, g] = 0; C[q, g] = S * rng.integers(0, L, (16, NC))
            elif o == 5:
                H[q, g] = 0; R[q, g] = np.where(R[q, g, :1] == 64, 64, 7 + (rng.random((1, NR)) < 0.1)); Z[q, g] = 7 + (rng.random((1, L)) < 0.1)
            elif o == 6:
                H[q, g] = 480; R[q, g] = np.where(R[q, g, :1] == 64, 64, 31 * rng.integers(0, 2, (1, NR))); Z[q, g] = 31 * rng.integers(0, 2, (1, L))
            else:
                w[q, g] = 255; C[q, g] = rng.choice(np.array([0, 1, S - 1, S, NR - S, NR - 2, NR - 1]), (16, NC))
                F[q, g] = 4095 * rng.integers(0, 2, L); P[q, g] = 4095 * rng.integers(0, 2, NR)
    return pack(w, R, C, P, Z, F, H)
def meet(rng):
    p = rng.integers(0, 4096, 1024)[:, None]; u = np.arange(1024)[None, :]
    c = ((p * u >> 5) + p) & (NC - 1); e = ((c * u >> 5) + c + 1) & (NC - 1); k = e[int(rng.integers(0, 1024)), int(rng.integers(512, 1024))]
    i, j = np.nonzero(e == k); o = rng.permutation(len(i)); i, j = i[o], j[o]
    x = np.resize(rng.permutation(np.unique(c[i, j], return_index=True)[1]), L); i, j = i[x], j[x]
    a, b = np.nonzero((e != k) & ~np.isin(c, c[i, j])); z = int(rng.integers(0, len(a)))
    return u[0, j], p[i, 0], int(u[0, b[z]]), int(p[a[z], 0])
def setup_inputs_crowd(rng):
    w, R, C, P, Z, F, H = parts(rng)
    for q in range(N):
        for g in range(8):
            o = (g + q) & 7; f0 = int(rng.integers(0, 4095))
            if q < 2:
                R[q, g] = 64; Z[q, g] = 0; F[q, g] = rng.permutation(NC)[:L]; H[q, g, 1] = int(rng.integers(220, 260))
            elif o <= 2:
                Z[q, g] = Z[q, g, :, :1].copy(); F[q, g] = f0; H[q, g, 0] = 480
                if o == 1: F[q, g, L - 1] = f0 + 1
                if o == 2: F[q, g, 1::2] = f0 + 1
            elif o <= 4:
                u, p, u1, p1 = meet(rng)
                if o == 4: u[L - 1] = u1; p[L - 1] = p1
                w[q, g] = 0; w[q, g, 0] = 1; w[q, g, 1] = 32; R[q, g] = 64; Z[q, g, 0] = u & 31; Z[q, g, 1] = u >> 5; F[q, g] = p
            elif o <= 6:
                w[q, g] = 0; R[q, g] = rng.integers(0, 4, (16, NR)); R[q, g, :, NR - 1] = 31; Z[q, g] = rng.integers(0, 4, (16, L)); F[q, g] = rng.permutation(NC)[:L]; H[q, g, 0] = 200
                C[q, g] = rng.integers(0, NR - 1, (16, NC)); C[q, g, rng.integers(0, 16, NC), np.arange(NC)] = NR - 1
                if o == 6: C[q, g, :, F[q, g, 3]] = rng.integers(0, NR - 1, 16)
            else:
                w[q, g] = 0; F[q, g] = f0; H[q, g, 0] = 150
    F[1, 7, L - 1] = F[1, 7, 0]
    return pack(w, R, C, P, Z, F, H)
def setup_inputs_ties(rng):
    w, R, C, P, Z, F, H = parts(rng)
    R = kill(rng, 8 * rng.integers(0, 2, (N, 8, 16, NR)), shares(rng)); Z = 8 * rng.integers(0, 2, (N, 8, 16, L)); H = 8 * rng.integers(4, 11, (N, 8, RO))
    C[:, :, 15] = np.where(rng.random((N, 8, NC)) < 0.3, C[:, :, 0], C[:, :, 15])
    return pack(w, R, C, P, Z, F, H)
def check_inputs(d):
    bad = []
    for k, lo, hi in (("rec", 0, 64), ("cel", 0, NR - 1), ("po", 0, 4095), ("pat", 0, 31), ("phi", 0, 4095), ("th", 0, 480), ("wt", 0, 255)):
        a = np.asarray(d[k]).astype(np.float64)
        if not (np.min(a) >= lo and np.max(a) <= hi and np.all(a == np.floor(a))): bad.append("range of " + k)
    a = np.asarray(d["rec"]).astype(np.float32).reshape(N, 8, 16, NR)
    if not np.all(np.all(a == 64, axis=2) | np.all(a <= 31, axis=2)): bad.append("a record of rec is neither living nor dead")
    return bad
def reference(rec, cel, po, pat, phi, th, wt):
    R = list(rec.astype(np.float32).astype(np.int32).reshape(N, 8, 16, NR)); C = list(cel.astype(np.int32).reshape(N, 8, 16, NC)); P = list(po.astype(np.int64))
    Z = list(pat.astype(np.float32).astype(np.int32).reshape(N, 8, 16, L)); F = list(phi.astype(np.int64))
    w = wt.astype(np.int32).reshape(N, 8, 16); H = th.astype(np.int64); A = [0] * N
    for t in range(RO):
        for q in range(N):
            R[q], C[q], P[q], Z[q], F[q], acc = visit(R[q], C[q], P[q], Z[q], F[q], w[q], H[q, :, t] + (A[q] & 31), t)
            A[q] = int(np.count_nonzero(acc))
        Z = [Z[(q - ST) % N] for q in range(N)]; F = [F[(q - ST) % N] for q in range(N)]
    return {"yrec": np.stack(R).reshape(N, 128, NR).astype(np.float32).astype(BF), "ycel": np.stack(C).reshape(N, 128, NC).astype(np.float32), "ypo": np.stack(P).astype(np.float32),
            "ypat": np.stack(Z).reshape(N, 128, L).astype(np.float32).astype(BF), "yphi": np.stack(F).astype(np.float32)}

from concourse.mybir import AluOpType as A, AxisListType as AX, ActivationFunctionType as F

SC = 131072.0
BIG = 8388608.0
M = 1.5 * 2.0 ** 40
CY, PE, WAKE = 0.00104, 0.0008, 0.06
f4, b2, h2, i4, u2 = "float32", "bfloat16", "float16", "int32", "uint16"
SB = {
    "rec_s": (2304, f4), "cel_s": (768, f4), "x": (4112, f4), "zr": (4096, b2), "ge": (4096, b2), "xi": (512, f4),
    "one": (128, f4), "e8": (128, f4), "e8h": (128, h2), "pi": (1, i4), "pi2": (1, i4), "mcol": (1, f4), "xr": (16, f4), "eq": (16, f4),
    "bmf": (128, f4), "bmh": (128, h2), "bmb": (128, b2), "pt": (64, f4), "px": (64, f4), "col": (8, f4), "c8": (8, f4), "c18": (4, f4), "zz": (8, f4),
    "red": (2048, b2), "w8": (2048, b2), "dig": (2048, b2), "sel": (2048, b2), "sp": (2048, b2), "bmp": (128, f4),
    "f_w8": (16, f4), "f_red": (16, f4), "f_dig": (16, f4),
    "wti": (1, i4), "wtf": (1, f4), "idf": (128, f4), "idb": (128, b2), "idh": (128, h2), "nib": (128, b2), "dlc": (128, h2),
    "trf": (128, f4), "trb": (128, b2), "oneh": (128, b2), "mi": (256, f4), "exc": (256, b2), "kc": (64, f4), "kr": (64, h2),
    "ncf": (256, f4), "nch": (512, h2), "m0": (256, f4), "ns": (256, f4), "sa": (256, f4), "d1": (256, f4), "dn": (256, f4),
    "lw": (16, f4), "clo": (32, f4), "nt": (32, f4), "ndc": (16, f4), "cdc": (16, f4), "dm": (32, f4), "vdc": (16, f4), "k15": (1, f4), "km": (1, f4),
    "rb": (2048, b2), "poi": (2048, i4), "poh": (2048, h2), "n8": (2048, b2), "n1": (2048, b2), "epo": (128, b2), "rown": (128, b2),
    "dg0": (2048, i4), "celi": (512, i4), "phi8": (256, i4), "ph8": (256, h2), "thi": (4, i4), "thh": (4, h2), "thf": (4, f4),
    "patb": (256, b2), "scr": (256, f4), "hw": (1, f4),
    "ui": (16, i4), "um": (16, i4), "u7i": (16, i4), "pht": (16, i4), "pu": (16, i4), "pv": (16, i4), "ci": (16, i4),
    "cei": (32, i4), "c1": (16, i4), "cu": (32, u2), "ceh": (32, b2), "sce": (512, u2), "ceb": (512, b2), "nbf": (256, f4), "nbh": (256, h2),
    "nv": (512, f4), "al": (256, f4), "vv": (256, f4), "dk": (256, f4), "tt": (256, f4), "ts": (256, f4),
    "ni": (32, i4), "cd": (32, i4), "hs": (32, f4), "o1": (32, f4), "o2": (32, f4), "ou": (32, u2), "xh": (256, f4), "xm": (256, f4), "pas": (16, b2),
    "dgb": (512, b2), "cf": (256, f4), "nc": (16, f4), "acc": (16, b2),
    "q1": (16, f4), "q2": (16, f4), "hd": (16, i4), "t1": (16, f4), "t2": (16, f4), "t3": (16, f4), "sl": (16, f4), "t5": (16, i4),
    "phh": (16, h2), "nd": (32, f4), "na": (32, f4), "nu": (32, u2), "kdh": (32, b2), "keh": (16, b2), "bd": (256, i4), "be": (256, i4), "bv": (256, f4),
    "dv": (256, f4), "vi": (16, i4), "vj": (16, i4), "vid": (16, f4), "vih": (16, h2), "vb": (256, h2), "fo": (16, f4), "vn": (16, f4), "vw": (16, f4), "va": (16, f4), "vu": (16, u2),
    "s1": (256, f4), "s2": (256, f4), "s3": (256, f4), "ka": (512, f4), "el": (256, f4), "es": (256, f4), "ek": (256, f4),
    "cnd": (16, b2), "ea": (16, f4), "eb": (16, f4), "eu": (16, u2), "asum": (1, f4), "ai": (1, i4), "h": (1, f4), "th_": (1, f4), "h5": (1, f4), "hk": (1, f4), "dh": (128, h2),
    "yb": (2048, b2), "yb2": (2048, b2), "dp8": (8, b2), "dgf": (2048, b2), "ypo_s": (2048, f4), "zo": (256, b2), "yph": (256, f4), "pho": (16, h2),
}
for _t in range(5):
    SB["z%d" % _t] = (256, b2)
    SB["ph%d" % _t] = (16, i4)
    if _t < 4:
        SB["zn%d" % _t] = (256, b2)
        SB["pn%d" % _t] = (16, i4)
ALIAS = {"yb": "rb", "yb2": "ge", "dgf": "zr_0", "dg0": "poi"}
TWICE = """zr ui um u7i pht pu pv ci cei c1 cu ceh sce ceb nbf nbh nv al vv dk tt ts ni cd hs o1 o2 ou pas dgb cf nc acc
q1 q2 hd t1 t2 t3 sl t5 phh nd na nu kdh keh vi vj vid vih vb fo vn vw va vu ka cnd ea eb eu asum ai h th_ h5 hk dh""".split()
for _n in TWICE:
    SB[_n + "_0"] = SB[_n + "_1"] = SB.pop(_n)
PLACE, SCRATCH, _al = {}, {}, {}
_fill = {f4: 0, b2: 0, h2: 0, i4: 0, u2: 0}
for _n in ALIAS:
    _al[_n] = SB.pop(_n)[0]
for _n, (_w, _d) in SB.items():
    PLACE[_n] = ("all_" + _d, _fill[_d], _w)
    _fill[_d] += (_w + 15) // 16 * 16
for _n, _o in ALIAS.items():
    PLACE[_n] = PLACE[_o][:2] + (_al[_n],)
for _d, _w in _fill.items():
    SCRATCH["all_" + _d] = ("sbuf", [128, _w], _d)
for _n in ("ab", "abe"):
    SCRATCH[_n] = ("sbuf", [128, 16, 16, 16], b2)
for _n in ("ee", "ev"):
    SCRATCH[_n] = ("sbuf", [128, 16, 272], b2)
for _k in range(8):
    SCRATCH["P%d" % _k] = ("psum", [128, 512], f4)
LOADS = ["rec", "cel", "po", "pat", "phi", "th", "wt"]
STORES = ["yrec", "ycel", "ypo", "ypat", "yphi"]
SEMAPHORES = ["qv", "qs", "qt", "qg"] + ["ld_" + k for k in LOADS] + ["st_" + k for k in STORES] + [a + str(t) for a in ("zl", "zr", "pl", "pr") for t in range(4)]
ORDER = []


def rank_program(g, core, T, topo):
    rank = T.rank_of(core)
    if rank is None:
        return
    dst = T.cores[(rank + 5) % 8]
    src = T.cores[(rank - 5) % 8]
    ENG = {"v": g.vector, "s": g.scalar, "t": g.tensor, "g": g, "y": g.sync}
    QS = {"v": "qv", "s": "qs", "t": "qt", "g": "qg"}
    ops, log, vis = [], {}, [0]

    def R(n, lo=0, hi=None, st=1, p=128):
        n = n + "_%d" % (vis[0] & 1) if n in TWICE else n
        tn, o, w = PLACE[n] if n in PLACE else (n, 0, 512)
        hi = w if hi is None else hi
        return (T[tn][0:p, o + lo:o + hi:st] if st != 1 else T[tn][0:p, o + lo:o + hi], [(tn, o + lo, o + hi, (o + lo) % 16 if st == 16 else -1)])

    def I(win, off):
        return (win[0].indirect(off[0]), win[1], off[1], 16 * (off[1][0][2] - off[1][0][1]))

    def do(e, fn, outs, ins, cost, tok=None, lat=0.0):
        writes = [r for o in outs for r in o[1]]
        reads = [r for i in ins if isinstance(i, tuple) for r in i[1]]
        reads += [r for x in list(outs) + list(ins) if isinstance(x, tuple) and len(x) > 2 for r in x[2]]
        n, deps = len(ops), {}
        for regs, iswr in ((reads, False), (writes, True)):
            for tn, lo, hi, ph in regs:
                ps = tn[0] == "P"
                for (a, b, w, d, eng, pb) in log.get(tn, ()):
                    over = a < hi and lo < b and (ph < 0 or pb < 0 or ph == pb)
                    if (over and (w or iswr)) or (ps and (eng != e or (e == "t" and w))):
                        deps[d] = deps.get(d, False) or not (eng == e and (e == "t" and ps or not over))
        for tn, lo, hi, ph in writes:
            log[tn] = [x for x in log.get(tn, []) if not (lo <= x[0] and x[1] <= hi and ph in (-1, x[5]) and (tn[0] != "P" or x[4] == e))]
            log[tn].append((lo, hi, True, n, e, ph))
        for tn, lo, hi, ph in reads:
            log[tn] = [x for x in log.get(tn, []) if not (not x[2] and x[4] == e and lo <= x[0] and x[1] <= hi and ph in (-1, x[5]))]
            log[tn].append((lo, hi, False, n, e, ph))
        ops.append((e, fn, deps, cost, tok, lat))

    def plan():
        n = len(ops)
        succ, left, prio, at_ = [[] for _ in ops], [len(o[2]) for o in ops], [0.0] * n, [0.0] * n
        for i, o in enumerate(ops):
            for d in o[2]:
                succ[d].append(i)
        for i in range(n - 1, -1, -1):
            prio[i] = ops[i][3] + ops[i][5] + max([prio[j] for j in succ[i]] or [0.0])
        free, cand, order = {}, {}, []
        for i in range(n):
            if not left[i]:
                cand.setdefault(ops[i][0], []).append(i)
        while cand:
            s, e = min((max(free.get(e, 0.0), min(at_[i] for i in c)), e) for e, c in cand.items())
            i = max((i for i in cand[e] if at_[i] <= s), key=lambda i: (prio[i], -i))
            cand[e].remove(i)
            if not cand[e]:
                del cand[e]
            order.append(i)
            end = s + ops[i][3]
            free[e] = 0.0 if e == "net" else end
            for j in succ[i]:
                at_[j] = max(at_[j], end + ops[i][5] + (WAKE if ops[j][0] != e else 0.0))
                left[j] -= 1
                if not left[j]:
                    cand.setdefault(ops[j][0], []).append(j)
        return order

    def issue(order):
        cnt, know, snap, got = {q: 0 for q in QS}, {e: {} for e in ENG}, {}, {}
        for i in order:
            e, fn, deps, cost, tok, lat = ops[i]
            if e != "net":
                want = {}
                for d, hard in deps.items():
                    s, v = got[d]
                    if hard and know[e].get(s, 0) < v:
                        want[s] = max(want.get(s, 0), v)
                for s in sorted(want, key=lambda s: (s in QS.values(), s)):
                    if know[e].get(s, 0) >= want[s] or any(o != s and snap.get((o, want[o]), {}).get(s, 0) >= want[s] and know[e].get(o, 0) < want[o] for o in want):
                        continue
                    ENG[e].wait_ge(T.sem[s], want[s])
                    for k, x in list(snap.get((s, want[s]), {}).items()) + [(s, want[s])]:
                        know[e][k] = max(know[e].get(k, 0), x)
                inst = fn(ENG[e])
            if tok is None:
                cnt[e] += 1
                got[i] = (QS[e], cnt[e])
                inst.then_inc(T.sem[QS[e]], 1)
                snap[got[i]] = dict(know[e])
                snap[got[i]][QS[e]] = cnt[e]
            else:
                got[i] = tok
        for e in QS:
            if know["g"].get(QS[e], 0) < cnt[e]:
                g.wait_ge(T.sem[QS[e]], cnt[e])

    def ap(x):
        return x[0] if isinstance(x, tuple) else x

    def size(x):
        n = 1
        for k in x[0].shape[1:]:
            n *= k
        return n

    def vec(fn, o, ins, both=False, n=None):
        al = [x for x in [o] + ins if isinstance(x, tuple)]
        ind = [x for x in al if len(x) > 2]
        if ind:
            c = 0.05 + ind[0][3] * CY * (3.8 if len(o) > 2 else 1.56)
        else:
            n = n or size(o)
            wide = any(SCRATCH[x[1][0][0]][2] in (f4, i4) for x in al if size(x) > 1 or n == 1)
            c = 0.02 + max(64, n * (2 if both and not any(x[1][0][0][0] == "P" for x in al) else 1 if wide else 0.5)) * CY
        do("v", fn, [o], ins, c)

    def tt(o, a, b, op):
        vec(lambda q: q.tensor_tensor(ap(o), ap(a), ap(b), op), o, [a, b], True)

    def ts(o, a, s1, s2, op0, op1=None):
        if op1 is None:
            vec(lambda q: q.tensor_scalar(ap(o), ap(a), ap(s1), None, op0), o, [a, s1])
        else:
            vec(lambda q: q.tensor_scalar(ap(o), ap(a), ap(s1), ap(s2), op0, op1), o, [a, s1, s2])

    def cp(o, a):
        vec(lambda q: q.tensor_copy(ap(o), ap(a)), o, [a])

    def fill(o, c):
        vec(lambda q: q.memset(ap(o), c), o, [])

    def total(o, a):
        vec(lambda q: q.tensor_reduce(ap(o), ap(a), AX.X, A.add), o, [a], n=size(a))

    def scan(o, a, b, op0, op1, init=0.0):
        vec(lambda q: q.tensor_tensor_scan(ap(o), ap(a), ap(b), init, op0, op1), o, [a, b])

    def act(o, a, fn, bias=0.0, scale=1.0):
        c = 0.065 + a[3] * CY * 1.56 if len(a) > 2 else 0.06 + max(64, size(o)) * CY
        do("s", lambda q: q.activation(ap(o), ap(a), fn, bias=ap(bias), scale=ap(scale)), [o], [a, bias, scale], c)

    def mm(o, l, r, start, stop):
        do("t", lambda q: q.matmul(ap(o), ap(l), ap(r), start, stop), [o], [l, r], max(min(64, size(l)), size(r)) * PE)

    def iota(o, pat, base, cm, flag=True, ins=()):
        if flag:
            do("g", lambda q: q.iota(ap(o), pat, base, cm, allow_small_or_imprecise_dtypes=True), [o], ins, 0.15 + 2 * size(o) * CY)
        else:
            do("g", lambda q: q.iota(ap(o), pat, base, cm), [o], ins, 0.2)

    def aff(o, a, pat, op, fillc, base, cm):
        do("g", lambda q: q.affine_select(ap(o), ap(a), pat, op, fillc, base, cm), [o], [a], 0.2 + 2 * size(o) * CY)

    def load(e, n, o):
        do(e, lambda q: q.dma_start(ap(o), T[n][:]).then_inc(T.sem["ld_" + n], 16), [o], [], 0.1, ("ld_" + n, 16), 2.0)

    def store(e, n, i):
        do(e, lambda q: q.dma_start(T[n][:], ap(i)).then_inc(T.sem["st_" + n], 16), [], [i], 0.1, ("st_" + n, 16), 2.0)

    def send(n, buf, l, r, t):
        rid, pid = topo.addr(dst, core)
        a, land, mark = R(buf + str(t)), R(n + str(t + 1)), ("", [("sent" + r + str(t), 0, 1, -1)])
        do("g", lambda q: q.remote_dma(ap(land), ap(a), T.sem[r + str(t)], T.sem[l + str(t)], pid, rid, topo.mask(core, dst)), [mark], [a], 0.5, ("sent", 1))
        do("net", None, [land], [mark], 0.0, (r + str(t), len(topo.engines(src, core))), 2.5)

    def fam(buf, s2):
        ts(R("f_" + buf), R("one", 0, 16), s2, None, A.mult)
        for q in range(8):
            act(R(buf, 16 * q, 16 * q + 15 * 129 + 1, 129), R("f_" + buf), F.Copy, scale=R("bmf", 16 * q, 16 * q + 1))

    def blk(buf, m):
        return R(buf, 128 * m, 128 * m + 128)

    load("y", "pat", R("patb"))
    load("y", "wt", R("wti"))
    load("y", "rec", R("rb"))
    load("s", "phi", R("phi8", p=8))
    load("s", "th", R("thi", p=8))
    load("s", "po", R("poi", p=8))
    load("y", "cel", R("celi"))

    fill(R("one"), 1.0)
    iota(R("pi"), [[1, 1]], 0, 1, False)
    iota(R("xr"), [[1, 16]], 0, 0)
    aff(R("e8", p=8), R("one", p=8), [[1, 8], [0, 16]], A.is_equal, 0.0, 0, -1)
    aff(R("idf"), R("one"), [[1, 128]], A.is_equal, 0.0, 0, -1)
    iota(R("mi"), [[0, 16], [1, 16]], 0, 0)
    iota(R("n8", p=1), [[8, 256], [0, 8]], 0, 0, ins=[R("e8")])
    iota(R("n1", p=1), [[0, 256], [1, 8]], 0, 0, ins=[R("e8")])
    iota(R("dig"), [[0, 2048]], 0, 0, ins=[R("e8")])
    iota(R("lw"), [[16, 16]], 0, 0)
    iota(R("kc"), [[0, 4], [1, 16]], -16, 0)
    iota(R("ncf"), [[8, 256]], 0, 0)
    fill(R("w8"), 0.0)
    fill(R("red"), 0.0)
    ts(R("pi2"), R("pi"), 15, None, A.bitwise_and)
    cp(R("mcol"), R("pi2"))
    cp(R("e8h", p=8), R("e8", p=8))
    ts(R("eq"), R("xr"), R("mcol"), None, A.is_equal)
    mm(R("P0", 0, 128), R("e8h", p=8), R("e8h", p=8), True, True)
    cp(R("bmf"), R("P0", 0, 128))
    aff(R("trf"), R("bmf"), [[1, 128]], A.is_gt, 0.0, 0, -1)
    fill(R("pt"), 0.0)
    fill(R("c8"), 8.0)
    fill(R("c18"), 0.125)
    fill(R("zz"), 0.0)
    scan(R("pt", 0, 8), R("c8"), R("zz"), A.mult, A.add, 0.125)
    scan(R("pt", 16, 20), R("c18"), R("zz", 0, 4), A.mult, A.add, 8.0)
    cp(R("pt", 36, 40), R("pt", 16, 20))
    ts(R("pt", 48, 52), R("pt", 16, 20), -1.0, 0.5, A.add, A.mult)
    cp(R("pt", 52, 56), R("pt", 48, 52))
    ts(R("pt", 51, 52), R("pt", 51, 52), 4.0, None, A.add)
    for i in range(4):
        tt(R("px", 16 * i, 16 * i + 16), R("pt", 16 * i, 16 * i + 16), R("eq"), A.mult)
        total(R("col", i, i + 1), R("px", 16 * i, 16 * i + 16))
    COL = [R("col", i, i + 1) for i in range(4)]
    ts(R("wtf"), R("wti"), 1.0 / SC, None, A.mult)
    act(R("z0"), R("patb"), F.Copy, scale=SC)
    fam("w8", R("wtf"))
    fam("red", -1024.0)
    ts(R("ph8", p=8), R("phi8", p=8), -2048.0, None, A.add)
    ts(R("exc"), R("mi"), R("mcol"), -32768.0, A.not_equal, A.mult)
    cp(R("idb"), R("idf"))
    fill(R("sa"), 0.0)
    fill(R("sa", 0, 256, 16), -BIG)
    mm(R("P5", 0, 256), R("idb"), R("exc"), True, False)
    mm(R("P5", 0, 256), R("e8h", p=8), R("ph8", p=8), False, True)
    scan(R("scr"), R("sa"), R("P5", 0, 256), A.add, A.max)
    ts(R("ph0"), R("scr", 15, 256, 16), 2048.0, None, A.add)
    cp(R("thh", p=8), R("thi", p=8))
    mm(R("P0", 128, 132), R("e8h", p=8), R("thh", p=8), True, True)
    cp(R("thf"), R("P0", 128, 132))
    ts(R("poh", p=8), R("poi", p=8), -2048.0, None, A.add)
    for q in range(8):
        act(R("epo", 16 * q, 16 * q + 16, p=8), R("pt", 16, 32, p=8), F.Copy, scale=R("e8", 16 * q, 16 * q + 1, p=8))
        act(R("rown", 16 * q, 16 * q + 16, p=1), R("pt", 32, 48, p=1), F.Copy)
    for b in range(4):
        o, rs = R("P%d" % (b + 1)), R("P%d" % ((b + 5) % 8))
        s = (512 * b, 512 * b + 512)
        act(rs, R("rb", *s), F.Copy, scale=SC)
        mm(o, R("epo", p=8), R("poh", s[0], s[1], p=8), True, False)
        mm(o, R("rown", p=1), R("n8", s[0], s[1], p=1), False, False)
        mm(o, R("rown", p=1), R("n1", s[0], s[1], p=1), False, True)
        ts(R("dg0", *s), o, COL[3], None, A.add)
        ts(R("dg0", *s), R("dg0", *s), 7, None, A.bitwise_and)
        tt(R("rec_s", *s), rs, R("dg0", *s), A.add)
    cp(R("cel_s", 0, 512), R("celi"))
    fam("dig", COL[0])
    cp(R("bmh"), R("bmf"))
    cp(R("bmb"), R("bmf"))
    for q in range(8):
        ts(R("bmp", 16 * q, 16 * q + 16), R("pt", 16, 32), R("bmf", 16 * q, 16 * q + 1), None, A.mult)
    for m in range(16):
        act(blk("sel", m), R("bmf"), F.Copy, scale=R("eq", m, m + 1))
        act(blk("sp", m), R("bmp"), F.Copy, scale=R("eq", m, m + 1))
    cp(R("idh"), R("idf"))
    ts(R("nib"), R("idf"), -1.0 / SC, None, A.mult)
    ts(R("dlc"), R("idf"), COL[2], None, A.mult)
    cp(R("trb"), R("trf"))
    cp(R("oneh"), R("one"))
    ts(R("kc"), R("kc"), R("eq", 1, 2), None, A.mult)
    ts(R("hw"), R("eq", 0, 1), 1024.0, None, A.mult)
    ts(R("kr"), R("kc"), R("hw"), None, A.add)
    ts(R("nch", 0, 256), R("ncf"), 0.0, None, A.mult)
    cp(R("nch", 256, 512), R("ncf"))
    for n, c, d in (("m0", 1.0, 0.0), ("ns", 2.0, -BIG), ("d1", 0.03125, -1048576.0), ("dn", -1.0, -1048576.0)):
        fill(R(n), c)
        fill(R(n, 0, 256, 16), d)
    ts(R("lw"), R("lw"), R("mcol"), None, A.add)
    for lo, c, d in ((0, 16.0, 1025.0), (16, 18.0, 3.0)):
        ts(R("clo", lo, lo + 16), R("lw"), 16.0, c - 4096.0, A.mult, A.add)
        fill(R("nt", lo, lo + 16), d)
    ts(R("ndc"), R("lw"), 7.0, -2048.0, A.mult, A.add)
    ts(R("cdc"), R("lw"), -1.0, -512.0, A.mult, A.add)
    ts(R("vdc"), R("lw"), -1.0, -2048.0, A.mult, A.add)
    ts(R("dm", 0, 16), R("lw"), 2048.0, None, A.add)
    ts(R("dm", 16, 32), R("lw"), 512.0, None, A.add)
    ts(R("km"), R("mcol"), -1.0, 15.0, A.mult, A.add)
    ts(R("k15"), R("mcol"), -15.0, None, A.add)
    fill(R("x", 4096, 4112), 0.0)
    cp(R("h"), R("thf", 0, 1))

    def thresholds():
        act(R("th_"), R("h"), F.Identity, bias=-510.0 * 1024.0, scale=1024.0)
        act(R("h5"), R("h"), F.Copy, scale=5.0)
        act(R("hk"), R("eq", 0, 1), F.Identity, bias=R("eq", 1, 2), scale=R("h"))
        ts(R("dh"), R("bmh"), R("hk"), None, A.mult)
    thresholds()

    def spread(bank, lo, n, rhs, first=True, fam_="sel"):
        for m in range(16):
            mm(R(bank, lo + m, lo + 256 * n, 16), blk(fam_, m), rhs, first, first or m == 15)

    def pairs(bank, en, keysb, klo, keysw, wlo, ok):
        mm(R(bank, 0, 256), R("idb"), R("exc"), True, False)
        for j in range(16):
            w = 256 - 16 * j
            e = (T[en][:, j, 0:w], [(en, j, j + 1, -1)])
            ts(e, R(keysb, klo + 16 * j, klo + 256), R(keysw, wlo + j, wlo + j + 1), R(ok, j, j + 1), A.is_equal, A.mult)
            if j < 15:
                mm(R(bank, 16 * j + 16, 256), R("bmb"), (T[en][:, j, 16:w], [(en, j, j + 1, -1)]), False, False)
        mm(R(bank, 0, 256), R("trb"), (T[en][:, :, 0:16], [(en, 0, 16, -1)]), False, True)

    def lowest(bank, ok, out):
        scan(R("cf"), R("sa"), R(bank, 0, 256), A.add, A.max)
        ts(R("nc"), R("cf", 15, 256, 16), 0.5, None, A.is_lt)
        tt(R(out), R("nc"), R(ok), A.mult)

    def reduce_block(bank, abn, b):
        o = R(bank, 64 * b, 64 * b + 64)
        mm(o, R("dh"), R("kr"), True, False)
        for m in range(16):
            mm(o, blk("red", m), (T[abn][:, 4 * b:4 * b + 4, m, :], [(abn, 4 * b, 4 * b + 4, -1)]), False, m == 15)

    def sizes(abn, i, a, scale):
        act((T[abn][:, 2 * i:2 * i + 2, :, :], [(abn, 2 * i, 2 * i + 2, -1)]), a, F.Abs, scale=scale)

    for t in range(4):
        vis[0] = t
        z, ph = R("z%d" % t), R("ph%d" % t)
        for m in range(16):
            mm(R("P0", 0, 16), blk("w8", m), R("z%d" % t, m, 256, 16), m == 0, m == 15)
        for k in range(16):
            o = R("zr", k, 4096, 16)
            if k < 4:
                cp(o, z)
            elif k < 12:
                act(o, z, F.Copy)
            else:
                aff(o, z, [[0, 256]], A.is_gt, 0.0, 1, 0)
        if t:
            ts(R("pht"), ph, float(77 * t), None, A.add)
        cp(R("ui"), R("P0", 0, 16))
        ts(R("um"), R("ui"), 4095, None, A.bitwise_and)
        tt(R("pu"), ph, R("um"), A.mult)
        ts(R("pv"), R("pu"), 5, 511, A.arith_shift_right, A.bitwise_and)
        tt(R("ci"), R("pv"), R("pht") if t else ph, A.add)
        ts(R("cei", 0, 16), R("ci"), 511, None, A.bitwise_and)
        tt(R("pu"), R("cei", 0, 16), R("um"), A.mult)
        ts(R("c1"), R("cei", 0, 16), 1.0, None, A.add)
        ts(R("pv"), R("pu"), 5, 511, A.arith_shift_right, A.bitwise_and)
        tt(R("ci"), R("pv"), R("c1"), A.add)
        ts(R("cei", 16, 32), R("ci"), 511, None, A.bitwise_and)
        cp(R("cu"), R("cei"))
        cp(R("sce"), I(R("cel_s", 0, 512), R("cu")))
        ts(R("ceh"), R("cei"), -256.0, None, A.add)
        ts(R("u7i"), R("um"), 7, None, A.bitwise_and)
        cp(R("kdh", 16, 32), R("u7i"))
        spread("P5", 0, 2, R("ceh"))
        act(R("ceb"), R("P5"), F.Copy)
        for i in range(8):
            s = (512 * i, 512 * i + 512)
            tt(R("x", *s), I(R("rec_s", 0, 2048), R("sce", 32 * i, 32 * i + 32)), R("zr", *s), A.subtract)
            sizes("ab", i, R("x", *s), 1.0 / SC)
            if i & 1:
                reduce_block("P1", "ab", i // 2)
        for i in range(8):
            s = (512 * i, 512 * i + 512)
            act(R("ge", *s), I(R("rec_s", 0, 2048), R("sce", 256 + 32 * i, 288 + 32 * i)), F.Identity, scale=1.0 / SC)
            bank = R("P%d" % (3 + (i & 1)))
            mm(bank, R("idb"), R("ge", *s), True, False)
            mm(bank, R("nib"), R("zr", *s), False, True)
            sizes("abe", i, bank, 1.0)
            if i & 1:
                reduce_block("P2", "abe", i // 2)
        ts(R("t1"), ph, 5.0, None, A.mult)
        tt(R("t1"), R("t1"), R("um"), A.add)
        ts(R("q1"), ph, R("h5"), None, A.add)
        tt(R("q2"), R("q1"), R("t1"), A.subtract)
        tt(R("nd", 0, 16), R("ndc"), R("u7i"), A.add)
        tt(R("nd", 16, 32), R("cdc"), R("cei", 0, 16), A.add)
        ts(R("al"), R("P1", 0, 256), R("th_"), -1.0, A.is_ge, A.mult)
        tt(R("vv"), R("P1", 0, 256), R("al"), A.mult)
        act(R("P7", 0, 256), R("vv"), F.Relu, scale=-3.0)
        scan(R("nv", 0, 256), R("ns"), R("P1", 0, 256), A.add, A.max)
        tt(R("tt"), R("vv"), R("P7", 0, 256), A.subtract)
        scan(R("ts"), R("m0"), R("tt"), A.mult, A.add)
        ts(R("pas"), R("ts", 15, 256, 16), 700.0, None, A.is_le)
        pairs("P7", "ee", "ceb", 0, "ceh", 0, "pas")
        scan(R("nv", 256, 512), R("m0"), R("vv"), A.mult, A.max)
        ts(R("ni"), R("nv", 15, 512, 16), 2.0, None, A.add)
        ts(R("cd"), R("ni"), 1023, None, A.bitwise_and)
        tt(R("hs"), R("ni"), R("nt"), A.is_ge)
        tt(R("o1"), R("clo"), R("cd"), A.subtract)
        tt(R("o2"), R("o1"), R("hs"), A.mult)
        ts(R("ou"), R("o2"), 4096.0, None, A.add)
        act(R("xh"), I(R("x", 0, 4112), R("ou", 0, 16)), F.Identity, bias=4.0 - SC / 2, scale=0.5)
        act(R("xm"), R("xh"), F.Identity, bias=M)
        act(R("P6", 256, 512), R("xm"), F.Identity, bias=-M)
        act(R("xi"), I(R("x", 0, 4112), R("ou")), F.Identity, bias=M)
        act(R("xi"), R("xi"), F.Identity, bias=-M)
        tt(R("zn%d" % t), R("P6", 256, 512), z, A.add)
        send("z", "zn", "zl", "zr", t)
        act(R("P6", 256, 512), R("zn%d" % t), F.Copy)
        tt(R("dgb"), I(R("x", 0, 4112), R("ou")), R("xi"), A.subtract)
        for m in range(16):
            mm(R("P0", 16, 48), blk("dig", m), R("dgb", m, 512, 16), m == 0, m == 15)
        lowest("P7", "pas", "acc")
        ts(R("hd"), R("ni", 0, 16), 10, None, A.arith_shift_right)
        ts(R("t2"), R("hd"), -5.0, None, A.mult)
        tt(R("t2"), R("t2"), R("q2"), A.add)
        tt(R("sl"), R("acc"), R("hs", 0, 16), A.mult)
        tt(R("t3"), R("P0", 16, 32), R("t2"), A.add)
        cp(R("vi"), R("P0", 32, 48))
        tt(R("t3"), R("t3"), R("sl"), A.mult)
        tt(R("t5"), R("t3"), R("t1"), A.add)
        ts(R("pn%d" % t), R("t5"), 4095, None, A.bitwise_and)
        send("ph", "pn", "pl", "pr", t)
        ts(R("vj"), R("vi"), 12, None, A.arith_shift_right)
        cp(R("vih"), R("vj"))
        spread("P7", 256, 1, R("vih"))
        cp(R("vid"), R("vj"))
        tt(R("fo"), R("acc"), R("hs", 16, 32), A.mult)
        scan(R("dk"), R("d1"), R("al"), A.add, A.max)
        cp(R("kdh", 0, 16), R("dk", 15, 256, 16))
        mm(R("P5"), R("idh"), R("nch"), True, False)
        spread("P5", 0, 2, R("kdh"), first=False)
        ts(R("phh"), R("pn%d" % t), -2048.0, None, A.add)
        act(R("nbf"), R("P5", 256, 512), F.Copy)
        act(R("ka", 0, 256), R("P5", 0, 256), F.Abs, bias=R("k15"), scale=32.0)
        act(R("P5", 0, 256), R("ka", 0, 256), F.Sign)
        cp(R("vb"), R("P7", 256, 512))
        pairs("P1", "ev", "vb", 0, "vid", 0, "fo")
        cp(R("nbh"), R("nbf"))
        mm(R("P6", 0, 256), R("dlc"), R("nbh"), True, False)
        spread("P6", 0, 1, R("phh"), first=False, fam_="sp")
        tt(R("na", 0, 16), R("nd", 0, 16), R("acc"), A.mult)
        tt(R("na", 16, 32), R("nd", 16, 32), R("acc"), A.mult)
        tt(R("na"), R("na"), R("dm"), A.add)
        cp(R("nu"), R("na"))
        tt(R("s1"), I(R("cel_s", 0, 512), R("cu", 0, 16)), R("nbf"), A.subtract)
        tt(R("s2"), R("s1"), R("P5", 0, 256), A.mult)
        tt(I(R("cel_s"), R("nu", 16, 32)), R("s2"), R("nbf"), A.add)
        lowest("P1", "fo", "vw")
        tt(R("va"), R("vid"), R("vdc"), A.add)
        tt(R("va"), R("va"), R("vw"), A.mult)
        tt(R("vn"), R("va"), R("dm", 0, 16), A.add)
        cp(R("vu"), R("vn"))
        act(R("dv"), R("dgb", 256, 512), F.Identity, bias=64.0 * SC)
        cp(I(R("rec_s"), R("vu")), R("dv"))
        ts(R("bd"), R("P6", 0, 256), COL[3], None, A.add)
        ts(R("be"), R("bd"), 7, None, A.bitwise_and)
        tt(R("bv"), R("be"), R("P6", 256, 512), A.add)
        cp(I(R("rec_s"), R("nu", 0, 16)), R("bv"))
        ts(R("el"), R("P2", 0, 256), R("th_"), -32.0, A.is_ge, A.mult)
        scan(R("es"), R("sa"), R("P2", 0, 256), A.add, A.max)
        ts(R("cnd"), R("es", 15, 256, 16), 500.0, None, A.is_lt)
        tt(R("cnd"), R("cnd"), R("acc"), A.mult)
        scan(R("ek"), R("dn"), R("el"), A.add, A.max)
        cp(R("keh"), R("ek", 15, 256, 16))
        spread("P6", 0, 1, R("keh"))
        act(R("ka", 256, 512), R("P6", 0, 256), F.Abs, bias=R("km"))
        act(R("P6", 0, 256), R("ka", 256, 512), F.Sign)
        pairs("P3", "ee", "ceb", 256, "ceh", 16, "cnd")
        tt(R("eb"), R("cdc"), R("cei", 16, 32), A.add)
        tt(R("s3"), I(R("cel_s", 0, 512), R("cu", 16, 32)), R("nbf"), A.subtract)
        tt(R("s3"), R("s3"), R("P6", 0, 256), A.mult)
        lowest("P3", "cnd", "ea")
        tt(R("eb"), R("eb"), R("ea"), A.mult)
        tt(R("eb"), R("eb"), R("dm", 16, 32), A.add)
        cp(R("eu"), R("eb"))
        tt(I(R("cel_s"), R("eu")), R("s3"), R("nbf"), A.add)
        if t < 3:
            mm(R("P0", 48, 64), R("oneh"), R("acc"), True, True)
            total(R("asum"), R("P0", 48, 64))
            cp(R("ai"), R("asum"))
            ts(R("ai"), R("ai"), 31, None, A.bitwise_and)
            r = R("ai")
            vis[0] = t + 1
            tt(R("h"), r, R("thf", t + 1, t + 2), A.add)
            thresholds()
    act(R("yb"), R("rec_s", 0, 2048), F.Identity, bias=128.0, scale=1.0 / SC)
    act(R("yb2"), R("yb"), F.Identity, bias=-128.0)
    store("y", "yrec", R("yb2"))
    ts(R("hw"), R("mcol"), 4.0, COL[0], A.is_lt, A.mult)
    ts(R("dp8"), R("bmf", 0, 128, 16), R("hw"), None, A.mult)
    ts(R("pho"), R("ph4"), -2048.0, None, A.add)
    store("y", "ycel", R("cel_s", 0, 512))
    for b in range(4):
        s = (512 * b, 512 * b + 512)
        o = R("P%d" % (1 + b))
        ts(o, R("rec_s", *s), M, -M, A.add, A.add)
        tt(R("dgf", *s), R("rec_s", *s), o, A.subtract)
        mm(R("P%d" % (1 + b), 0, 512, p=8), R("dp8"), R("dgf", *s), True, True)
        act(R("ypo_s", s[0], s[1], p=8), R("P%d" % (1 + b), 0, 512, p=8), F.Copy)
    store("y", "ypo", R("ypo_s", p=8))
    act(R("zo"), R("z4"), F.Copy, scale=1.0 / SC)
    store("y", "ypat", R("zo"))
    for m in range(16):
        mm(R("P5", m, 256, 16, p=8), R("sel", 128 * m, 128 * m + 128, 16), R("pho"), True, True)
    act(R("yph", p=8), R("P5", 0, 256, p=8), F.Identity, bias=2048.0)
    store("y", "yphi", R("yph", p=8))
    if not ORDER:
        ORDER.extend(plan())
    issue(ORDER)
    for n in STORES:
        g.wait_ge(T.sem["st_" + n], 16)
    k = len(topo.engines(core, dst))
    for t in range(4):
        g.wait_ge(T.sem["zl%d" % t], k)
        g.wait_ge(T.sem["pl%d" % t], k)
